import numpy as np, ml_dtypes
CORES = [0,8,16,24,1,9,17,25,2,10,18,26,3,11,19,27]
N = 16
def setup_inputs(rng):
    return {"x": rng.standard_normal((N, 128, 16), dtype=np.float32).astype(ml_dtypes.bfloat16)}
def reference(x):
    s = x.sum(axis=0, dtype=np.float64).astype(x.dtype)
    b = 16 // N
    return {"y": np.stack([s[:, r * b:(r + 1) * b] for r in range(N)])}

@@ -1,0 +1,157 @@
+from concourse.bass import DstId, RemoteDMATransfer
+from concourse.mybir import AluOpType
+
+DRAM = False
+K = 1
+W = 16 // K
+FOLDERS = ((6, 0, ("mate", "own")),)
+W1_SPLIT = False
+W2_SPLIT = False
+FINAL = "acc_store"
+
+if DRAM:
+    SCRATCH = {
+        "xd": ("dram", [K, 128, W], "bfloat16"),
+        "slots": ("dram", [8, 128, W], "bfloat16"),
+        "part": ("dram", [2, K, 128, W], "bfloat16"),
+    }
+else:
+    SCRATCH = {
+        "xd": ("sbuf", [128, 16], "bfloat16"),
+        "slots": ("sbuf", [128, 128], "bfloat16"),
+        "part": ("sbuf", [128, 32], "bfloat16"),
+    }
+SEMAPHORES = ["loc", "gath", "pe", "po", "sent"]
+
+
+def bits(m):
+    return bin(m).count("1")
+
+
+def w1_plan(core):
+    c = core // 8
+    e = 8 // K
+    out = []
+    for s in range(K):
+        near = [8 * c + f for (f, fs, grp) in FOLDERS if fs == s and 8 * c + f != core]
+        far = [8 * (c ^ 2) + f for (f, fs, grp) in FOLDERS if fs == s]
+        lo = ((1 << e) - 1) << (s * e)
+        if W1_SPLIT:
+            out.append((s, lo, far))
+            out.append((s, lo << 8, near))
+        else:
+            out.append((s, lo, far + near))
+    return out
+
+
+def w2_plan(core):
+    c, k = divmod(core, 8)
+    out = []
+    for (f, s, grp) in FOLDERS:
+        if f != k:
+            continue
+        mate = [(8 * (c ^ 1) + j, 1) for j in range(4)]
+        own = [(8 * c + j, 0) for j in range(4)]
+        if "mate" in grp and "own" in grp:
+            if W2_SPLIT:
+                out.append((s, 0x00FF, "po", mate))
+                out.append((s, 0xFF00, "pe", own))
+            else:
+                out.append((s, 0x00FF, "pe", mate + own))
+        elif "mate" in grp:
+            out.append((s, 0x00FF, "po", mate))
+        else:
+            out.append((s, 0xFFFF, "pe", own))
+    return out
+
+
+def rank_program(g, core, T, topo):
+    rank = T.rank_of(core)
+    c, k = divmod(core, 8)
+    folds = w2_plan(core) if c < 4 else []
+    if rank is None and not folds:
+        return
+
+    def did(dst):
+        rid, pid, se = topo.addr(dst)
+        return DstId(rid=rid, pnc=pid)
+
+    def xd(s):
+        return T.xd[s] if DRAM else T.xd[:, :]
+
+    def slot(i):
+        return T.slots[i] if DRAM else T.slots[:, 16 * i:16 * i + 16]
+
+    def part(p, s):
+        return T.part[p, s] if DRAM else T.part[:, 16 * p:16 * p + 16]
+
+    def col(p, d):
+        if not DRAM:
+            return T.part[:, 16 * p + d:16 * p + d + 1]
+        if K == 1:
+            return T.part[p, 0, :, d:d + 1]
+        return T.part[p, :, (d // W)::K, (d % W):(d % W) + 1]
+
+    sems = {"pe": T.sem.pe, "po": T.sem.po}
+    sent = 0
+    nloc = 0
+
+    if rank is not None:
+        g.dma_start(out=T.xd[:], in_=T.x[:]).then_inc(T.sem.loc, 16)
+        nloc += 16
+        g.wait_ge(T.sem.loc, nloc)
+        i = (c >> 1) * 4 + k
+        trs = []
+        for (s, m, dsts) in w1_plan(core):
+            trs.append(RemoteDMATransfer(dst_ids=[did(t) for t in dsts], dma_engine_mask=m, remote_sem=T.sem.gath,
+                                         srcs=[xd(s)], dsts=[slot(i) for t in dsts], alu_op=0))
+            sent += bits(m)
+        g.remote_dma_fused(trs, local_sem=T.sem.sent)
+
+    if folds:
+        need = 0
+        for r in T.cores:
+            for (s, m, dsts) in w1_plan(r):
+                need += bits(m) * dsts.count(core)
+        g.wait_ge(T.sem.gath, need)
+        trs = []
+        for (s, m, name, dsts) in folds:
+            srcs = []
+            for i in range(8):
+                src_core = 8 * ((c & 1) + 2 * (i // 4)) + i % 4
+                srcs.append(xd(s) if src_core == core else slot(i))
+            trs.append(RemoteDMATransfer(dst_ids=[did(t) for (t, p) in dsts], dma_engine_mask=m, remote_sem=sems[name],
+                                         srcs=srcs, dsts=[part(p, s) for (t, p) in dsts], alu_op=1))
+            sent += bits(m)
+        g.remote_dma_fused(trs, local_sem=T.sem.sent)
+
+    if rank is not None:
+        need = {"pe": 0, "po": 0}
+        for f in range(32):
+            for (s, m, name, dsts) in w2_plan(f):
+                need[name] += bits(m) * [t for (t, p) in dsts].count(core)
+        slow = {"allow_slow_non_contiguous": True} if DRAM else {}
+        if FINAL == "acc_store":
+            for name in ("pe", "po"):
+                if need[name]:
+                    g.wait_ge(sems[name], need[name])
+            if DRAM:
+                g.dma_start(out=T.part[0], in_=T.part[1], accum_op=AluOpType.add).then_inc(T.sem.loc, 16)
+            else:
+                g.dma_start(out=col(0, rank), in_=col(1, rank), accum_op=AluOpType.add).then_inc(T.sem.loc, 16)
+            nloc += 16
+            g.wait_ge(T.sem.loc, nloc)
+            g.dma_start(out=T.y[:], in_=col(0, rank), **slow).then_inc(T.sem.loc, 16)
+            nloc += 16
+            g.wait_ge(T.sem.loc, nloc)
+        else:
+            g.wait_ge(sems["pe"], need["pe"])
+            g.dma_start(out=T.y[:], in_=col(0, rank), **slow).then_inc(T.sem.loc, 16)
+            nloc += 16
+            g.wait_ge(sems["po"], need["po"])
+            g.wait_ge(T.sem.loc, nloc)
+            g.dma_start(out=T.y[:], in_=col(1, rank), accum_op=AluOpType.add, **slow).then_inc(T.sem.loc, 16)
+            nloc += 16
+            g.wait_ge(T.sem.loc, nloc)
+
+    g.wait_ge(T.sem.sent, sent)

@@ -1,7 +1,7 @@
 from concourse.bass import DstId, RemoteDMATransfer
 from concourse.mybir import AluOpType
 
-DRAM = False
+DRAM = True
 K = 1
 W = 16 // K
 FOLDERS = ((6, 0, ("mate", "own")),)

@@ -2,11 +2,11 @@ from concourse.bass import DstId, RemoteDMATransfer
 from concourse.mybir import AluOpType
 
 DRAM = True
-K = 1
+K = 2
 W = 16 // K
-FOLDERS = ((6, 0, ("mate", "own")),)
-W1_SPLIT = False
-W2_SPLIT = False
+FOLDERS = ((6, 0, ("mate", "own")), (7, 1, ("mate", "own")))
+W1_SPLIT = True
+W2_SPLIT = True
 FINAL = "acc_store"
 
 if DRAM:

@@ -1,157 +1,54 @@
 from concourse.bass import DstId, RemoteDMATransfer
 from concourse.mybir import AluOpType
 
-DRAM = True
 K = 2
 W = 16 // K
-FOLDERS = ((6, 0, ("mate", "own")), (7, 1, ("mate", "own")))
-W1_SPLIT = True
-W2_SPLIT = True
-FINAL = "acc_store"
+FOLD = (6, 7)
+E1 = 8 // K
 
-if DRAM:
-    SCRATCH = {
-        "xd": ("dram", [K, 128, W], "bfloat16"),
-        "slots": ("dram", [8, 128, W], "bfloat16"),
-        "part": ("dram", [2, K, 128, W], "bfloat16"),
-    }
-else:
-    SCRATCH = {
-        "xd": ("sbuf", [128, 16], "bfloat16"),
-        "slots": ("sbuf", [128, 128], "bfloat16"),
-        "part": ("sbuf", [128, 32], "bfloat16"),
-    }
-SEMAPHORES = ["loc", "gath", "pe", "po", "sent"]
-
-
-def bits(m):
-    return bin(m).count("1")
-
-
-def w1_plan(core):
-    c = core // 8
-    e = 8 // K
-    out = []
-    for s in range(K):
-        near = [8 * c + f for (f, fs, grp) in FOLDERS if fs == s and 8 * c + f != core]
-        far = [8 * (c ^ 2) + f for (f, fs, grp) in FOLDERS if fs == s]
-        lo = ((1 << e) - 1) << (s * e)
-        if W1_SPLIT:
-            out.append((s, lo, far))
-            out.append((s, lo << 8, near))
-        else:
-            out.append((s, lo, far + near))
-    return out
-
-
-def w2_plan(core):
-    c, k = divmod(core, 8)
-    out = []
-    for (f, s, grp) in FOLDERS:
-        if f != k:
-            continue
-        mate = [(8 * (c ^ 1) + j, 1) for j in range(4)]
-        own = [(8 * c + j, 0) for j in range(4)]
-        if "mate" in grp and "own" in grp:
-            if W2_SPLIT:
-                out.append((s, 0x00FF, "po", mate))
-                out.append((s, 0xFF00, "pe", own))
-            else:
-                out.append((s, 0x00FF, "pe", mate + own))
-        elif "mate" in grp:
-            out.append((s, 0x00FF, "po", mate))
-        else:
-            out.append((s, 0xFFFF, "pe", own))
-    return out
+SCRATCH = {
+    "xd": ("dram", [K, 128, W], "bfloat16"),
+    "slots": ("dram", [8, 128, W], "bfloat16"),
+    "part": ("dram", [2, K, 128, W], "bfloat16"),
+}
+SEMAPHORES = ["loc", "gath", "arr", "sent"]
 
 
 def rank_program(g, core, T, topo):
     rank = T.rank_of(core)
     c, k = divmod(core, 8)
-    folds = w2_plan(core) if c < 4 else []
-    if rank is None and not folds:
-        return
 
     def did(dst):
         rid, pid, se = topo.addr(dst)
         return DstId(rid=rid, pnc=pid)
 
-    def xd(s):
-        return T.xd[s] if DRAM else T.xd[:, :]
-
-    def slot(i):
-        return T.slots[i] if DRAM else T.slots[:, 16 * i:16 * i + 16]
-
-    def part(p, s):
-        return T.part[p, s] if DRAM else T.part[:, 16 * p:16 * p + 16]
-
-    def col(p, d):
-        if not DRAM:
-            return T.part[:, 16 * p + d:16 * p + d + 1]
-        if K == 1:
-            return T.part[p, 0, :, d:d + 1]
-        return T.part[p, :, (d // W)::K, (d % W):(d % W) + 1]
-
-    sems = {"pe": T.sem.pe, "po": T.sem.po}
-    sent = 0
-    nloc = 0
-
     if rank is not None:
         g.dma_start(out=T.xd[:], in_=T.x[:]).then_inc(T.sem.loc, 16)
-        nloc += 16
-        g.wait_ge(T.sem.loc, nloc)
+        g.wait_ge(T.sem.loc, 16)
         i = (c >> 1) * 4 + k
         trs = []
-        for (s, m, dsts) in w1_plan(core):
-            trs.append(RemoteDMATransfer(dst_ids=[did(t) for t in dsts], dma_engine_mask=m, remote_sem=T.sem.gath,
-                                         srcs=[xd(s)], dsts=[slot(i) for t in dsts], alu_op=0))
-            sent += bits(m)
-        g.remote_dma_fused(trs, local_sem=T.sem.sent)
-
-    if folds:
-        need = 0
-        for r in T.cores:
-            for (s, m, dsts) in w1_plan(r):
-                need += bits(m) * dsts.count(core)
-        g.wait_ge(T.sem.gath, need)
-        trs = []
-        for (s, m, name, dsts) in folds:
-            srcs = []
-            for i in range(8):
-                src_core = 8 * ((c & 1) + 2 * (i // 4)) + i % 4
-                srcs.append(xd(s) if src_core == core else slot(i))
-            trs.append(RemoteDMATransfer(dst_ids=[did(t) for (t, p) in dsts], dma_engine_mask=m, remote_sem=sems[name],
-                                         srcs=srcs, dsts=[part(p, s) for (t, p) in dsts], alu_op=1))
-            sent += bits(m)
-        g.remote_dma_fused(trs, local_sem=T.sem.sent)
-
-    if rank is not None:
-        need = {"pe": 0, "po": 0}
-        for f in range(32):
-            for (s, m, name, dsts) in w2_plan(f):
-                need[name] += bits(m) * [t for (t, p) in dsts].count(core)
-        slow = {"allow_slow_non_contiguous": True} if DRAM else {}
-        if FINAL == "acc_store":
-            for name in ("pe", "po"):
-                if need[name]:
-                    g.wait_ge(sems[name], need[name])
-            if DRAM:
-                g.dma_start(out=T.part[0], in_=T.part[1], accum_op=AluOpType.add).then_inc(T.sem.loc, 16)
-            else:
-                g.dma_start(out=col(0, rank), in_=col(1, rank), accum_op=AluOpType.add).then_inc(T.sem.loc, 16)
-            nloc += 16
-            g.wait_ge(T.sem.loc, nloc)
-            g.dma_start(out=T.y[:], in_=col(0, rank), **slow).then_inc(T.sem.loc, 16)
-            nloc += 16
-            g.wait_ge(T.sem.loc, nloc)
-        else:
-            g.wait_ge(sems["pe"], need["pe"])
-            g.dma_start(out=T.y[:], in_=col(0, rank), **slow).then_inc(T.sem.loc, 16)
-            nloc += 16
-            g.wait_ge(sems["po"], need["po"])
-            g.wait_ge(T.sem.loc, nloc)
-            g.dma_start(out=T.y[:], in_=col(1, rank), accum_op=AluOpType.add, **slow).then_inc(T.sem.loc, 16)
-            nloc += 16
-            g.wait_ge(T.sem.loc, nloc)
-
-    g.wait_ge(T.sem.sent, sent)
+        for s in range(K):
+            dsts = [8 * (c ^ 2) + FOLD[s], 8 * c + FOLD[s]]
+            trs.append(RemoteDMATransfer(dst_ids=[did(t) for t in dsts], dma_engine_mask=((1 << E1) - 1) << (s * E1),
+                                         remote_sem=T.sem.gath, srcs=[T.xd[s]], dsts=[T.slots[i] for t in dsts],
+                                         alu_op=0))
+        g.remote_dma_fused(trs, local_sem=T.sem.arr)
+        g.wait_ge(T.sem.arr, K * E1 + 2 * K * 8)
+        g.dma_start(out=T.part[0], in_=T.part[1], accum_op=AluOpType.add).then_inc(T.sem.loc, 16)
+        g.wait_ge(T.sem.loc, 32)
+        g.dma_start(out=T.y[:], in_=T.part[0, :, (rank // W)::K, (rank % W):(rank % W) + 1],
+                    allow_slow_non_contiguous=True).then_inc(T.sem.loc, 16)
+        g.wait_ge(T.sem.loc, 48)
+    elif c < 4 and k in FOLD:
+        s = FOLD.index(k)
+        g.wait_ge(T.sem.gath, 8 * E1)
+        srcs = [T.slots[i] for i in range(8)]
+        mate = [8 * (c ^ 1) + j for j in range(4)]
+        own = [8 * c + j for j in range(4)]
+        g.remote_dma_fused([
+            RemoteDMATransfer(dst_ids=[did(t) for t in mate], dma_engine_mask=0x00FF, remote_sem=T.sem.arr,
+                              srcs=srcs, dsts=[T.part[1, s] for t in mate], alu_op=1),
+            RemoteDMATransfer(dst_ids=[did(t) for t in own], dma_engine_mask=0xFF00, remote_sem=T.sem.arr,
+                              srcs=srcs, dsts=[T.part[0, s] for t in own], alu_op=1),
+        ], local_sem=T.sem.sent)
+        g.wait_ge(T.sem.sent, 16)

from concourse.bass import DstId, RemoteDMATransfer
from concourse.mybir import AluOpType

K = 2
W = 16 // K
FOLD = (6, 7)
E1 = 8 // K

SCRATCH = {
    "xd": ("dram", [K, 128, W], "bfloat16"),
    "slots": ("dram", [8, 128, W], "bfloat16"),
    "part": ("dram", [2, K, 128, W], "bfloat16"),
}
SEMAPHORES = ["loc", "gath", "arr", "sent"]


def rank_program(g, core, T, topo):
    rank = T.rank_of(core)
    c, k = divmod(core, 8)

    def did(dst):
        rid, pid, se = topo.addr(dst)
        return DstId(rid=rid, pnc=pid)

    if rank is not None:
        g.dma_start(out=T.xd[:], in_=T.x[:]).then_inc(T.sem.loc, 16)
        g.wait_ge(T.sem.loc, 16)
        i = (c >> 1) * 4 + k
        trs = []
        for s in range(K):
            dsts = [8 * (c ^ 2) + FOLD[s], 8 * c + FOLD[s]]
            trs.append(RemoteDMATransfer(dst_ids=[did(t) for t in dsts], dma_engine_mask=((1 << E1) - 1) << (s * E1),
                                         remote_sem=T.sem.gath, srcs=[T.xd[s]], dsts=[T.slots[i] for t in dsts],
                                         alu_op=0))
        g.remote_dma_fused(trs, local_sem=T.sem.arr)
        g.wait_ge(T.sem.arr, K * E1 + 2 * K * 8)
        g.dma_start(out=T.part[0], in_=T.part[1], accum_op=AluOpType.add).then_inc(T.sem.loc, 16)
        g.wait_ge(T.sem.loc, 32)
        g.dma_start(out=T.y[:], in_=T.part[0, :, (rank // W)::K, (rank % W):(rank % W) + 1],
                    allow_slow_non_contiguous=True).then_inc(T.sem.loc, 16)
        g.wait_ge(T.sem.loc, 48)
    elif c < 4 and k in FOLD:
        s = FOLD.index(k)
        g.wait_ge(T.sem.gath, 8 * E1)
        srcs = [T.slots[i] for i in range(8)]
        mate = [8 * (c ^ 1) + j for j in range(4)]
        own = [8 * c + j for j in range(4)]
        g.remote_dma_fused([
            RemoteDMATransfer(dst_ids=[did(t) for t in mate], dma_engine_mask=0x00FF, remote_sem=T.sem.arr,
                              srcs=srcs, dsts=[T.part[1, s] for t in mate], alu_op=1),
            RemoteDMATransfer(dst_ids=[did(t) for t in own], dma_engine_mask=0xFF00, remote_sem=T.sem.arr,
                              srcs=srcs, dsts=[T.part[0, s] for t in own], alu_op=1),
        ], local_sem=T.sem.sent)
        g.wait_ge(T.sem.sent, 16)
